import numpy as np
import ml_dtypes


def mxq(x, axis, fmt="e4m3"):
    dtype, down = {"e4m3": (ml_dtypes.float8_e4m3fn, 7), "e5m2": (ml_dtypes.float8_e5m2, 14)}[fmt]
    v = np.moveaxis(np.asarray(x, np.float32).astype(ml_dtypes.bfloat16).astype(np.float64), axis, -1)
    blocks = v.reshape(v.shape[:-1] + (-1, 32))
    amax = np.abs(blocks).max(-1, keepdims=True)
    byte = np.maximum(np.where(amax > 0, np.frexp(amax)[1] - 1 + 127, 0) - down, 1)
    scale = np.exp2(byte - 127.0)
    codes = (blocks / scale).astype(np.float32).astype(dtype).astype(np.float64)
    return np.moveaxis((codes * scale).reshape(v.shape), -1, axis)


WIDE = False


def mx_kscale(k):
    if not WIDE:
        return np.ones(k)
    levels = np.array([10, -10, 5, -5, 0])
    if k % 512:
        return np.exp2(np.random.permutation(np.resize(levels, k // 32))).repeat(32)
    a = np.empty((k // 512, 16))
    for p in range(k // 512):
        a[p, :8] = np.random.permutation(np.resize(levels, 8))
        for g in range(8):
            far = levels[np.abs(levels - a[p, g]) >= 10]
            a[p, g + 8] = far[np.random.randint(len(far))]
    return np.exp2(a.ravel()).repeat(32)


def f64(x):
    return np.asarray(x).astype(np.float64)


def striped(idx):
    return np.tile(idx.reshape(-1, 16).T, (8, 1)).astype(np.uint16)


def unstriped(offs):
    return offs[:16].T.reshape(-1).astype(np.int64)


def pack_weight(w):
    k, n = w.shape
    w = f64(np.asarray(w, np.float32).astype(ml_dtypes.bfloat16)).reshape(k // 32, 32, n)
    amax = np.abs(w).max(1)
    byte = np.clip(np.where(amax > 0, np.frexp(amax)[1] - 1 + 127 - 7, 1), 1, 254)
    scaled = (w * np.exp2(127.0 - byte)[:, None, :]).reshape(k, n).astype(np.float32)
    words = np.ascontiguousarray(scaled.reshape(k // 512, 128, 4, n).transpose(0, 1, 3, 2)).astype(ml_dtypes.float8_e4m3fn).view(np.uint8)
    return words, np.ascontiguousarray(byte.astype(np.uint8).reshape(k // 512, 16, n))


def unpack_weight(words, scales):
    g, p, n, _ = words.shape
    vals = np.ascontiguousarray(words).view(ml_dtypes.float8_e4m3fn).astype(np.float64) * np.repeat(np.exp2(scales.astype(np.float64) - 127.0), 8, axis=1)[..., None]
    return vals.transpose(0, 1, 3, 2).reshape(g * 512, n)


def relu(v):
    return np.maximum(v, 0.0)

def planes(y):
    n, m = y.shape
    v = y.astype(np.float32).astype(ml_dtypes.bfloat16).astype(np.float64).reshape(n // 32, 32, m)
    top = np.abs(v).max(1)
    byte = np.clip(np.where(top > 0, np.frexp(top)[1] - 1 + 127 - 7, 1), 1, 254)
    codes = (v * np.exp2(127.0 - byte)[:, None, :]).reshape(n, m).astype(np.float32).astype(ml_dtypes.float8_e4m3fn).view(np.uint8)
    words = codes.reshape(n // 512, 128, 4, m).transpose(0, 1, 3, 2)
    return np.ascontiguousarray(words), np.ascontiguousarray(byte.astype(np.uint8).reshape(n // 512, 16, m))


K, T, H = 512, 512, 512


def setup_inputs():
    n = np.random.standard_normal
    s = mx_kscale(K)[:, None]
    u = mx_kscale(H)
    packed_xT = pack_weight(n((K, T)) * s)
    return {
        "x_words": packed_xT[0],
        "x_scales": packed_xT[1],
        "w1": (n((K, H)) / np.sqrt(K) / s * u).astype(np.float32),
        "w2": (n((H, H)) / np.sqrt(2 * H) / u[:, None]).astype(np.float32),
        "w3": (n((H, H)) / np.sqrt(2 * H) / u[:, None]).astype(np.float32),
        "pos1": striped(np.random.permutation(T)),
        "pos2": striped(np.random.permutation(T)),
        "pos3": striped(np.random.permutation(T)),
    }


def reference(x_words, x_scales, w1, w2, w3, pos1, pos2, pos3):
    xq = unpack_weight(x_words, x_scales)
    h = relu(mxq(f64(w1), 0, "e4m3").T @ xq)
    z = np.maximum(np.maximum(h[:, unstriped(pos1)], h[:, unstriped(pos2)]), h[:, unstriped(pos3)])
    out_0 = relu(mxq(f64(w2), 0, "e4m3").T @ mxq(h, 0, "e4m3") + mxq(f64(w3), 0, "e4m3").T @ mxq(z, 0, "e4m3"))
    return (out_0,) + planes(out_0)

@@ -1,0 +1,222 @@
+from contextlib import ExitStack
+
+import concourse.mybir as mybir
+
+K, T, H = 512, 512, 512
+FLOPS = 3 * 2 * 512 * 512 * 512
+
+F32 = mybir.dt.float32
+BF16 = mybir.dt.bfloat16
+I32 = mybir.dt.int32
+U32 = mybir.dt.uint32
+U16 = mybir.dt.uint16
+U8 = mybir.dt.uint8
+FP8X4 = mybir.dt.float8_e4m3fn_x4
+RELU = mybir.ActivationFunctionType.Relu
+COPY = mybir.ActivationFunctionType.Copy
+MAX = mybir.AluOpType.max
+
+P = 128
+PACK = 4
+UNIT = 128
+
+
+def tile_picked_wsagecat_maxrelu_lo_kernel(
+    tc, x_words, x_scales, w1, w2, w3, pos1, pos2, pos3, out_0, out_1, out_2
+):
+    nc = tc.nc
+    with ExitStack() as ctx:
+        keep = ctx.enter_context(tc.tile_pool(name="keep", bufs=1))
+        psum = ctx.enter_context(tc.psum_pool(name="psum", bufs=1))
+
+        def half(tag, width):
+            return keep.tile([P, width], BF16, name=tag, tag=tag, align_bytes=64)
+
+        def mx_tiles(name, width):
+            codes = keep.tile([P, width], U32, name=name + "_codes", align_bytes=64)
+            scales = keep.tile([P, width], U8, name=name + "_scales", align_bytes=64)
+            return codes, scales
+
+        def quantise(mx, first, staged):
+            cols = slice(first, first + staged.shape[1] // PACK)
+            nc.vector.quantize_mx(out=mx[0][:, cols].bitcast(FP8X4), scales=mx[1][:, cols], in_=staged)
+
+        def product(acc, weights, t, moving, cols, start, stop):
+            dealt = slice(P * t, P * (t + 1))
+            nc.tensor.matmul_mx(
+                out=acc,
+                lhsT=weights[0][:, dealt].bitcast(FP8X4),
+                lhsT_scale=weights[1][:, dealt],
+                rhs=moving[0][:, cols].bitcast(FP8X4),
+                rhs_scale=moving[1][:, cols],
+                start=start,
+                stop=stop,
+            )
+
+        raw = [keep.tile([P, PACK, H], F32, name="raw%d" % i) for i in range(3)]
+        lists = [keep.tile([P, T // 16], U16, name="list%d" % i) for i in range(3)]
+        xq = mx_tiles("x", T)
+        nc.sync.dma_start(out=raw[0][:], in_=w1.rearrange("(p j) c -> p j c", j=PACK))
+        scale_rows = x_scales[0].bitcast(I32)
+        for q in range(4):
+            nc.scalar.dma_start(
+                out=xq[1][32 * q : 32 * (q + 1), :].bitcast(I32),
+                in_=scale_rows[4 * q : 4 * q + 4, :].partition_broadcast(8),
+            )
+        nc.sync.dma_start(out=xq[0][:].bitcast(I32), in_=x_words[0].rearrange("p c r -> p (c r)").bitcast(I32))
+        nc.sync.dma_start(lists[0][:], pos1)
+        nc.sync.dma_start(lists[1][:], pos2)
+        nc.sync.dma_start(lists[2][:], pos3)
+        nc.sync.dma_start(out=raw[1][:], in_=w2.rearrange("(p j) c -> p j c", j=PACK))
+        nc.sync.dma_start(out=raw[2][:], in_=w3.rearrange("(p j) c -> p j c", j=PACK))
+
+        def deal_views(staged, source, t0, t1):
+            dst = staged[:].rearrange("p (t m j) -> p m j t", t=t1 - t0, j=PACK)
+            src = source[:].rearrange("p j (m t) -> p m j t", t=PACK)[:, :, :, t0:t1]
+            return dst, src
+
+        w1q = mx_tiles("w1", H)
+        w1_lo = half("w1_lo", 2 * H)
+        w1_hi = half("w1_hi", 2 * H)
+        dst, src = deal_views(w1_lo, raw[0], 0, 2)
+        nc.vector.tensor_copy(out=dst, in_=src)
+        dst, src = deal_views(w1_hi, raw[0], 2, 4)
+        nc.scalar.activation(out=dst, in_=src, func=COPY)
+        quantise(w1q, 0, w1_lo[:, 0:H])
+        quantise(w1q, P, w1_lo[:, H : 2 * H])
+        quantise(w1q, 2 * P, w1_hi[:])
+
+        h = keep.tile([P, PACK, T], F32, name="h")
+        for t in range(PACK):
+            bank = psum.tile([P, T], F32, name="h_bank", tag="plane%d" % t)
+            product(bank[:], w1q, t, xq, slice(0, T), True, True)
+            nc.scalar.activation(out=h[:, t, :], in_=bank[:], func=RELU)
+
+        def weave_views(staged, planes):
+            dst = staged.rearrange("p (c i t) -> p c t i", i=4, t=PACK)
+            src = planes.rearrange("p t (c i) -> p c t i", i=4)
+            return dst, src
+
+        def gather(tile, d, t, first, n):
+            dst = tile[:].rearrange("p (a t b) -> p a t b", a=2, t=PACK)[:, :, t, :]
+            offsets = lists[d][:, first // 16 : (first + n) // 16]
+            nc.vector.tensor_copy(out=dst, in_=h[:, t, :].indirect(offsets))
+
+        def z_views(staged, z):
+            dst = staged[:].rearrange("p (a c i t) -> p a c t i", a=2, i=4, t=PACK)
+            src = z[:].rearrange("p (a t c i) -> p a c t i", a=2, i=4, t=PACK)
+            return dst, src
+
+        def largest(name, early, late_a, late_b, width):
+            pair = half(name + "_pair", width)
+            nc.vector.tensor_tensor(out=pair[:], in0=late_a[:], in1=late_b[:], op=MAX)
+            z = half(name, width)
+            nc.vector.tensor_tensor(out=z[:], in0=pair[:], in1=early[:], op=MAX)
+            return z
+
+        hq = mx_tiles("h", T)
+        zq = mx_tiles("z", T)
+        w2q = mx_tiles("w2", H)
+        w3q = mx_tiles("w3", H)
+        yq = mx_tiles("y", T)
+        out_rows = out_0.rearrange("(p t) v -> p t v", t=PACK)
+        word_rows = out_1[0].rearrange("p c r -> p (c r)").bitcast(I32)
+
+        def unit(u, staged):
+            cols = slice(UNIT * u, UNIT * (u + 1))
+            bank = psum.tile([P, PACK, UNIT], F32, name="y_bank", tag="unit%d" % u)
+            for t in range(PACK):
+                product(bank[:, t, :], w2q, t, hq, cols, True, False)
+                product(bank[:, t, :], w3q, t, zq, cols, False, True)
+            y = keep.tile([P, PACK, UNIT], F32, name="y%d" % u)
+            nc.scalar.activation(out=y[:], in_=bank[:], func=RELU)
+            nc.sync.dma_start(out=out_rows[:, :, cols], in_=y[:])
+            nc.scalar.activation(
+                out=staged.rearrange("p (v t) -> p v t", t=PACK), in_=bank[:].rearrange("p t v -> p v t"), func=RELU
+            )
+
+        g0 = [half("g0_%d" % d, PACK * 256) for d in range(3)]
+        for t in range(PACK):
+            for d in range(3):
+                gather(g0[d], d, t, 0, 256)
+        z0 = largest("z0", g0[2], g0[0], g0[1], PACK * 256)
+
+        h_st = half("h_st", PACK * T)
+        dst, src = weave_views(h_st[:], h[:])
+        nc.scalar.copy(out=dst, in_=src)
+        quantise(hq, 0, h_st[:])
+
+        w2_st = half("w2_st", PACK * H)
+        dst, src = deal_views(w2_st, raw[1], 0, 4)
+        nc.scalar.activation(out=dst, in_=src, func=COPY)
+        quantise(w2q, 0, w2_st[:])
+
+        w3_st = half("w3_st", PACK * H)
+        dst, src = deal_views(w3_st, raw[2], 0, 4)
+        nc.scalar.activation(out=dst, in_=src, func=COPY)
+        quantise(w3q, 0, w3_st[:])
+
+        z0_st = half("z0_st", PACK * 256)
+        dst, src = z_views(z0_st, z0)
+        nc.scalar.copy(out=dst, in_=src)
+        quantise(zq, 0, z0_st[:])
+
+        last = slice(3 * UNIT, 4 * UNIT)
+        last_banks = [psum.tile([P, UNIT], F32, name="last_bank", tag="plane%d" % t) for t in range(PACK)]
+        for t in range(PACK):
+            product(last_banks[t][:], w2q, t, hq, last, True, False)
+
+        g1 = [half(tag, PACK * UNIT) for tag in ("w2_st", "w3_st", "z0_st")]
+        for d in range(3):
+            for t in range(PACK):
+                gather(g1[d], d, t, 256, UNIT)
+        z1 = largest("z1", g1[0], g1[1], g1[2], PACK * UNIT)
+
+        y01_st = half("y01_st", PACK * 256)
+        unit(0, y01_st[:, 0:512])
+        unit(1, y01_st[:, 512:1024])
+        quantise(yq, 0, y01_st[:])
+        nc.sync.dma_start(out=word_rows[:, 0:256], in_=yq[0][:, 0:256].bitcast(I32))
+
+        z1_st = half("z1_st", PACK * UNIT)
+        dst, src = z_views(z1_st, z1)
+        nc.scalar.copy(out=dst, in_=src)
+        quantise(zq, 256, z1_st[:])
+
+        y2_st = half("y2_st", PACK * UNIT)
+        unit(2, y2_st[:])
+        quantise(yq, 256, y2_st[:])
+
+        g2 = [half(tag, PACK * UNIT) for tag in ("w3_st", "z1_st", "y01_st")]
+        for d in range(2):
+            for t in range(PACK):
+                gather(g2[d], d, t, 384, UNIT)
+        pair = half("z2_pair", PACK * UNIT)
+        gather(g2[2], 2, 0, 384, UNIT)
+        nc.vector.tensor_tensor(out=pair[:], in0=g2[0][:], in1=g2[1][:], op=MAX)
+        for t in range(1, PACK):
+            gather(g2[2], 2, t, 384, UNIT)
+        z2 = half("z2", PACK * UNIT)
+        nc.vector.tensor_tensor(out=z2[:], in0=pair[:], in1=g2[2][:], op=MAX)
+        z2_st = half("z2_st", PACK * UNIT)
+        dst, src = z_views(z2_st, z2)
+        nc.vector.tensor_copy(out=dst, in_=src)
+        quantise(zq, 384, z2_st[:])
+
+        y3 = keep.tile([P, PACK, UNIT], F32, name="y3")
+        for t in range(PACK):
+            product(last_banks[t][:], w3q, t, zq, last, False, True)
+            if t % 2 == 0:
+                nc.scalar.activation(out=y3[:, t, :], in_=last_banks[t][:], func=RELU)
+            else:
+                nc.vector.tensor_scalar_max(out=y3[:, t, :], in0=last_banks[t][:], scalar1=0.0)
+        nc.sync.dma_start(out=out_rows[:, :, last], in_=y3[:])
+        y3_st = half("y3_st", PACK * UNIT)
+        dst, src = weave_views(y3_st[:], y3[:])
+        nc.vector.tensor_copy(out=dst, in_=src)
+        quantise(yq, 384, y3_st[:])
+        nc.sync.dma_start(out=word_rows[:, 256:512], in_=yq[0][:, 256:512].bitcast(I32))
+        out_scale_rows = out_2[0].bitcast(I32)
+        for q in range(4):
+            queue = nc.scalar if q % 2 == 0 else nc.sync
+            queue.dma_start(out=out_scale_rows[4 * q : 4 * q + 4, :], in_=yq[1][32 * q : 32 * q + 4, :].bitcast(I32))

@@ -97,22 +97,10 @@ def tile_picked_wsagecat_maxrelu_lo_kernel(
             src = planes.rearrange("p t (c i) -> p c t i", i=4)
             return dst, src
 
-        def gather(tile, d, t, first, n):
-            dst = tile[:].rearrange("p (a t b) -> p a t b", a=2, t=PACK)[:, :, t, :]
+        def gather(tile, d, t, first, n, run):
+            dst = tile[:].rearrange("p (a t b) -> p a t b", b=run, t=PACK)[:, :, t, :]
             offsets = lists[d][:, first // 16 : (first + n) // 16]
             nc.vector.tensor_copy(out=dst, in_=h[:, t, :].indirect(offsets))
-
-        def z_views(staged, z):
-            dst = staged[:].rearrange("p (a c i t) -> p a c t i", a=2, i=4, t=PACK)
-            src = z[:].rearrange("p (a t c i) -> p a c t i", a=2, i=4, t=PACK)
-            return dst, src
-
-        def largest(name, early, late_a, late_b, width):
-            pair = half(name + "_pair", width)
-            nc.vector.tensor_tensor(out=pair[:], in0=late_a[:], in1=late_b[:], op=MAX)
-            z = half(name, width)
-            nc.vector.tensor_tensor(out=z[:], in0=pair[:], in1=early[:], op=MAX)
-            return z
 
         hq = mx_tiles("h", T)
         zq = mx_tiles("z", T)
@@ -135,11 +123,18 @@ def tile_picked_wsagecat_maxrelu_lo_kernel(
                 out=staged.rearrange("p (v t) -> p v t", t=PACK), in_=bank[:].rearrange("p t v -> p v t"), func=RELU
             )
 
-        g0 = [half("g0_%d" % d, PACK * 256) for d in range(3)]
+        W = PACK * UNIT
+        g0 = [half("g0_%d" % d, 3 * W) for d in range(3)]
         for t in range(PACK):
             for d in range(3):
-                gather(g0[d], d, t, 0, 256)
-        z0 = largest("z0", g0[2], g0[0], g0[1], PACK * 256)
+                gather(g0[d], d, t, 0, 3 * UNIT, UNIT)
+        pair = half("pair0", 3 * W)
+        z = half("z0", 3 * W)
+        blocks = [slice(W * u, W * (u + 1)) for u in range(3)]
+        for b in blocks:
+            nc.vector.tensor_tensor(out=pair[:, b], in0=g0[0][:, b], in1=g0[1][:, b], op=MAX)
+        for b in blocks:
+            nc.vector.tensor_tensor(out=z[:, b], in0=pair[:, b], in1=g0[2][:, b], op=MAX)
 
         h_st = half("h_st", PACK * T)
         dst, src = weave_views(h_st[:], h[:])
@@ -156,52 +151,42 @@ def tile_picked_wsagecat_maxrelu_lo_kernel(
         nc.scalar.activation(out=dst, in_=src, func=COPY)
         quantise(w3q, 0, w3_st[:])
 
-        z0_st = half("z0_st", PACK * 256)
-        dst, src = z_views(z0_st, z0)
-        nc.scalar.copy(out=dst, in_=src)
-        quantise(zq, 0, z0_st[:])
-
         last = slice(3 * UNIT, 4 * UNIT)
         last_banks = [psum.tile([P, UNIT], F32, name="last_bank", tag="plane%d" % t) for t in range(PACK)]
         for t in range(PACK):
             product(last_banks[t][:], w2q, t, hq, last, True, False)
 
-        g1 = [half(tag, PACK * UNIT) for tag in ("w2_st", "w3_st", "z0_st")]
-        for d in range(3):
-            for t in range(PACK):
-                gather(g1[d], d, t, 256, UNIT)
-        z1 = largest("z1", g1[0], g1[1], g1[2], PACK * UNIT)
+        for u in range(3):
+            z_st = half("z_st%d" % u, W)
+            dst, src = weave_views(z_st[:], z[:, blocks[u]].rearrange("p (t v) -> p t v", t=PACK))
+            nc.scalar.copy(out=dst, in_=src)
+            quantise(zq, UNIT * u, z_st[:])
 
-        y01_st = half("y01_st", PACK * 256)
-        unit(0, y01_st[:, 0:512])
-        unit(1, y01_st[:, 512:1024])
-        quantise(yq, 0, y01_st[:])
-        nc.sync.dma_start(out=word_rows[:, 0:256], in_=yq[0][:, 0:256].bitcast(I32))
-
-        z1_st = half("z1_st", PACK * UNIT)
-        dst, src = z_views(z1_st, z1)
-        nc.scalar.copy(out=dst, in_=src)
-        quantise(zq, 256, z1_st[:])
-
-        y2_st = half("y2_st", PACK * UNIT)
-        unit(2, y2_st[:])
-        quantise(yq, 256, y2_st[:])
-
-        g2 = [half(tag, PACK * UNIT) for tag in ("w3_st", "z1_st", "y01_st")]
+        g1 = [half("z_st%d" % d, W) for d in range(3)]
         for d in range(2):
             for t in range(PACK):
-                gather(g2[d], d, t, 384, UNIT)
-        pair = half("z2_pair", PACK * UNIT)
-        gather(g2[2], 2, 0, 384, UNIT)
-        nc.vector.tensor_tensor(out=pair[:], in0=g2[0][:], in1=g2[1][:], op=MAX)
+                gather(g1[d], d, t, 384, UNIT, UNIT // 2)
+        pair1 = half("pair1", W)
+        gather(g1[2], 2, 0, 384, UNIT, UNIT // 2)
+        nc.vector.tensor_tensor(out=pair1[:], in0=g1[0][:], in1=g1[1][:], op=MAX)
         for t in range(1, PACK):
-            gather(g2[2], 2, t, 384, UNIT)
-        z2 = half("z2", PACK * UNIT)
-        nc.vector.tensor_tensor(out=z2[:], in0=pair[:], in1=g2[2][:], op=MAX)
-        z2_st = half("z2_st", PACK * UNIT)
-        dst, src = z_views(z2_st, z2)
-        nc.vector.tensor_copy(out=dst, in_=src)
-        quantise(zq, 384, z2_st[:])
+            gather(g1[2], 2, t, 384, UNIT, UNIT // 2)
+        z1 = half("z1", W)
+        z3_st = half("z3_st", W)
+        halves = [slice(0, W // 2), slice(W // 2, W)]
+        for b in halves:
+            nc.vector.tensor_tensor(out=z1[:, b], in0=pair1[:, b], in1=g1[2][:, b], op=MAX)
+        for b in halves:
+            dst, src = weave_views(z3_st[:, b], z1[:, b].rearrange("p (t v) -> p t v", t=PACK))
+            nc.vector.tensor_copy(out=dst, in_=src)
+        for a in range(2):
+            quantise(zq, 384 + 64 * a, z3_st[:, halves[a]])
+
+        for u in range(3):
+            y_st = half("y_st%d" % u, W)
+            unit(u, y_st[:])
+            quantise(yq, UNIT * u, y_st[:])
+        nc.sync.dma_start(out=word_rows[:, 0:256], in_=yq[0][:, 0:256].bitcast(I32))
 
         y3 = keep.tile([P, PACK, UNIT], F32, name="y3")
         for t in range(PACK):

@@ -19,6 +19,7 @@ MAX = mybir.AluOpType.max
 P = 128
 PACK = 4
 UNIT = 128
+SPARE = 192
 
 
 def tile_picked_wsagecat_maxrelu_lo_kernel(
@@ -53,10 +54,12 @@ def tile_picked_wsagecat_maxrelu_lo_kernel(
                 stop=stop,
             )
 
-        raw = [keep.tile([P, PACK, H], F32, name="raw%d" % i) for i in range(3)]
+        w1_raw = [keep.tile([P, 2, H], F32, name="w1_raw%d" % i) for i in range(2)]
+        raw = [keep.tile([P, PACK, H], F32, name="raw%d" % i) for i in range(2)]
         lists = [keep.tile([P, T // 16], U16, name="list%d" % i) for i in range(3)]
         xq = mx_tiles("x", T)
-        nc.sync.dma_start(out=raw[0][:], in_=w1.rearrange("(p j) c -> p j c", j=PACK))
+        for i in range(2):
+            nc.sync.dma_start(out=w1_raw[i][:], in_=w1.rearrange("(p j) c -> p j c", j=PACK)[:, 2 * i : 2 * i + 2, :])
         scale_rows = x_scales[0].bitcast(I32)
         for q in range(4):
             nc.scalar.dma_start(
@@ -67,27 +70,34 @@ def tile_picked_wsagecat_maxrelu_lo_kernel(
         nc.sync.dma_start(lists[0][:], pos1)
         nc.sync.dma_start(lists[1][:], pos2)
         nc.sync.dma_start(lists[2][:], pos3)
-        nc.sync.dma_start(out=raw[1][:], in_=w2.rearrange("(p j) c -> p j c", j=PACK))
-        nc.sync.dma_start(out=raw[2][:], in_=w3.rearrange("(p j) c -> p j c", j=PACK))
+        nc.sync.dma_start(out=raw[0][:], in_=w2.rearrange("(p j) c -> p j c", j=PACK))
+        nc.sync.dma_start(out=raw[1][:], in_=w3.rearrange("(p j) c -> p j c", j=PACK))
 
         def deal_views(staged, source, t0, t1):
-            dst = staged[:].rearrange("p (t m j) -> p m j t", t=t1 - t0, j=PACK)
+            dst = staged.rearrange("p (t m j) -> p m j t", t=t1 - t0, j=PACK)
             src = source[:].rearrange("p j (m t) -> p m j t", t=PACK)[:, :, :, t0:t1]
             return dst, src
 
         w1q = mx_tiles("w1", H)
-        w1_lo = half("w1_lo", 2 * H)
-        w1_hi = half("w1_hi", 2 * H)
-        dst, src = deal_views(w1_lo, raw[0], 0, 2)
-        nc.vector.tensor_copy(out=dst, in_=src)
-        dst, src = deal_views(w1_hi, raw[0], 2, 4)
-        nc.scalar.activation(out=dst, in_=src, func=COPY)
-        quantise(w1q, 0, w1_lo[:, 0:H])
-        quantise(w1q, P, w1_lo[:, H : 2 * H])
-        quantise(w1q, 2 * P, w1_hi[:])
+        w1_st = [half("w1_st01", 2 * H), half("w1_st23", 2 * H)]
+        for i in range(2):
+            dst, src = deal_views(w1_st[1][:], w1_raw[i], 2, 4)
+            nc.vector.tensor_copy(out=dst[:, :, 2 * i : 2 * i + 2, :], in_=src)
+            dst, src = deal_views(w1_st[0][:], w1_raw[i], 0, 2)
+            nc.scalar.activation(out=dst[:, :, 2 * i : 2 * i + 2, :], in_=src, func=COPY)
+        quantise(w1q, 3 * P, w1_st[1][:, H : 2 * H])
+        quantise(w1q, 2 * P, w1_st[1][:, 0:H])
+        quantise(w1q, 0, w1_st[0][:])
 
-        h = keep.tile([P, PACK, T], F32, name="h")
-        for t in range(PACK):
+        h_flat = keep.tile([P, PACK * T + SPARE], F32, name="h_flat")
+        nc.gpsimd.memset(h_flat[:, PACK * T :], 0.0)
+        h = h_flat[:, 0 : PACK * T].rearrange("p (t v) -> p t v", t=PACK)
+        for a in range(2):
+            cols = slice(a * T // 2, (a + 1) * T // 2)
+            bank = psum.tile([P, T // 2], F32, name="h_bank", tag=("plane3", "spare")[a])
+            product(bank[:], w1q, 3, xq, cols, True, True)
+            nc.scalar.activation(out=h[:, 3, cols], in_=bank[:], func=RELU)
+        for t in (2, 1, 0):
             bank = psum.tile([P, T], F32, name="h_bank", tag="plane%d" % t)
             product(bank[:], w1q, t, xq, slice(0, T), True, True)
             nc.scalar.activation(out=h[:, t, :], in_=bank[:], func=RELU)
@@ -98,14 +108,13 @@ def tile_picked_wsagecat_maxrelu_lo_kernel(
             return dst, src
 
         def gather(tile, d, t, first, n, run):
-            dst = tile[:].rearrange("p (a t b) -> p a t b", b=run, t=PACK)[:, :, t, :]
+            dst = tile.rearrange("p (a t b) -> p a t b", b=run, t=PACK)[:, :, t, :]
             offsets = lists[d][:, first // 16 : (first + n) // 16]
-            nc.vector.tensor_copy(out=dst, in_=h[:, t, :].indirect(offsets))
+            nc.vector.tensor_copy(out=dst, in_=h_flat[:, T * t : T * (t + 1) + (SPARE if n == T else 0)].indirect(offsets))
 
         hq = mx_tiles("h", T)
-        zq = mx_tiles("z", T)
-        w2q = mx_tiles("w2", H)
-        w3q = mx_tiles("w3", H)
+        zq = mx_tiles("z", 3 * UNIT)
+        w23q = mx_tiles("w23", 2 * H)
         yq = mx_tiles("y", T)
         out_rows = out_0.rearrange("(p t) v -> p t v", t=PACK)
         word_rows = out_1[0].rearrange("p c r -> p (c r)").bitcast(I32)
@@ -114,8 +123,8 @@ def tile_picked_wsagecat_maxrelu_lo_kernel(
             cols = slice(UNIT * u, UNIT * (u + 1))
             bank = psum.tile([P, PACK, UNIT], F32, name="y_bank", tag="unit%d" % u)
             for t in range(PACK):
-                product(bank[:, t, :], w2q, t, hq, cols, True, False)
-                product(bank[:, t, :], w3q, t, zq, cols, False, True)
+                product(bank[:, t, :], w23q, t, hq, cols, True, False)
+                product(bank[:, t, :], w23q, PACK + t, zq, cols, False, True)
             y = keep.tile([P, PACK, UNIT], F32, name="y%d" % u)
             nc.scalar.activation(out=y[:], in_=bank[:], func=RELU)
             nc.sync.dma_start(out=out_rows[:, :, cols], in_=y[:])
@@ -124,73 +133,86 @@ def tile_picked_wsagecat_maxrelu_lo_kernel(
             )
 
         W = PACK * UNIT
-        g0 = [half("g0_%d" % d, 3 * W) for d in range(3)]
-        for t in range(PACK):
+        g0 = [half("g0_%d" % d, (4 if d == 0 else 3) * W) for d in range(3)]
+        for t in (3, 2, 1, 0):
             for d in range(3):
-                gather(g0[d], d, t, 0, 3 * UNIT, UNIT)
+                gather(g0[d][:], d, t, 0, (4 if d == 0 else 3) * UNIT, UNIT)
         pair = half("pair0", 3 * W)
         z = half("z0", 3 * W)
-        blocks = [slice(W * u, W * (u + 1)) for u in range(3)]
-        for b in blocks:
+        parts = [slice(0, 2 * W), slice(2 * W, 3 * W)]
+        for b in parts:
             nc.vector.tensor_tensor(out=pair[:, b], in0=g0[0][:, b], in1=g0[1][:, b], op=MAX)
-        for b in blocks:
+        for b in parts:
             nc.vector.tensor_tensor(out=z[:, b], in0=pair[:, b], in1=g0[2][:, b], op=MAX)
 
         h_st = half("h_st", PACK * T)
-        dst, src = weave_views(h_st[:], h[:])
+        dst, src = weave_views(h_st[:], h)
         nc.scalar.copy(out=dst, in_=src)
         quantise(hq, 0, h_st[:])
 
-        w2_st = half("w2_st", PACK * H)
-        dst, src = deal_views(w2_st, raw[1], 0, 4)
-        nc.scalar.activation(out=dst, in_=src, func=COPY)
-        quantise(w2q, 0, w2_st[:])
-
-        w3_st = half("w3_st", PACK * H)
-        dst, src = deal_views(w3_st, raw[2], 0, 4)
-        nc.scalar.activation(out=dst, in_=src, func=COPY)
-        quantise(w3q, 0, w3_st[:])
+        w23_st = half("w23_st", 2 * PACK * H)
+        for i in range(2):
+            dst, src = deal_views(w23_st[:, i * PACK * H : (i + 1) * PACK * H], raw[i], 0, 4)
+            nc.scalar.activation(out=dst, in_=src, func=COPY)
+        quantise(w23q, 0, w23_st[:])
 
         last = slice(3 * UNIT, 4 * UNIT)
         last_banks = [psum.tile([P, UNIT], F32, name="last_bank", tag="plane%d" % t) for t in range(PACK)]
         for t in range(PACK):
-            product(last_banks[t][:], w2q, t, hq, last, True, False)
+            product(last_banks[t][:], w23q, t, hq, last, True, False)
 
+        z01_st = half("z01_st", 2 * W)
+        nc.scalar.copy(
+            out=z01_st[:].rearrange("p (u c i t) -> p u c t i", u=2, i=4, t=PACK),
+            in_=z[:, parts[0]].rearrange("p (u t c i) -> p u c t i", u=2, i=4, t=PACK),
+        )
+        quantise(zq, 0, z01_st[:])
+        z2_st = half("z2_st", W)
+        dst, src = weave_views(z2_st[:], z[:, parts[1]].rearrange("p (t v) -> p t v", t=PACK))
+        nc.scalar.copy(out=dst, in_=src)
+        quantise(zq, 2 * UNIT, z2_st[:])
+
+        y_st = [half("y_st%d" % u, W) for u in range(3)]
         for u in range(3):
-            z_st = half("z_st%d" % u, W)
-            dst, src = weave_views(z_st[:], z[:, blocks[u]].rearrange("p (t v) -> p t v", t=PACK))
-            nc.scalar.copy(out=dst, in_=src)
-            quantise(zq, UNIT * u, z_st[:])
+            unit(u, y_st[u][:])
+            quantise(yq, UNIT * u, y_st[u][:])
+        nc.sync.dma_start(out=word_rows[:, 0:256], in_=yq[0][:, 0:256].bitcast(I32))
 
-        g1 = [half("z_st%d" % d, W) for d in range(3)]
-        for d in range(2):
-            for t in range(PACK):
-                gather(g1[d], d, t, 384, UNIT, UNIT // 2)
+        g1 = [None, half("z01_st", W)[:], half("z2_st", W)[:]]
+        for t in range(PACK):
+            gather(g1[1], 1, t, 384, UNIT, UNIT // 2)
         pair1 = half("pair1", W)
         gather(g1[2], 2, 0, 384, UNIT, UNIT // 2)
-        nc.vector.tensor_tensor(out=pair1[:], in0=g1[0][:], in1=g1[1][:], op=MAX)
+        nc.vector.tensor_tensor(
+            out=pair1[:].rearrange("p (a t b) -> p a t b", a=2, t=PACK),
+            in0=g0[0][:, 3 * W : 4 * W].rearrange("p (t a b) -> p a t b", a=2, t=PACK),
+            in1=g1[1].rearrange("p (a t b) -> p a t b", a=2, t=PACK),
+            op=MAX,
+        )
         for t in range(1, PACK):
             gather(g1[2], 2, t, 384, UNIT, UNIT // 2)
         z1 = half("z1", W)
-        z3_st = half("z3_st", W)
-        halves = [slice(0, W // 2), slice(W // 2, W)]
-        for b in halves:
-            nc.vector.tensor_tensor(out=z1[:, b], in0=pair1[:, b], in1=g1[2][:, b], op=MAX)
-        for b in halves:
-            dst, src = weave_views(z3_st[:, b], z1[:, b].rearrange("p (t v) -> p t v", t=PACK))
-            nc.vector.tensor_copy(out=dst, in_=src)
-        for a in range(2):
-            quantise(zq, 384 + 64 * a, z3_st[:, halves[a]])
 
-        for u in range(3):
-            y_st = half("y_st%d" % u, W)
-            unit(u, y_st[:])
-            quantise(yq, UNIT * u, y_st[:])
-        nc.sync.dma_start(out=word_rows[:, 0:256], in_=yq[0][:, 0:256].bitcast(I32))
+        def planes(flat, t0, t1):
+            return flat.rearrange("p (a t b) -> p a t b", a=2, t=PACK)[:, :, t0:t1, :]
+
+        for t0, t1 in ((0, 3), (3, 4)):
+            nc.vector.tensor_tensor(
+                out=planes(z1[:], t0, t1), in0=planes(pair1[:], t0, t1), in1=planes(g1[2], t0, t1), op=MAX
+            )
+        z3_st = half("y_st0", W)
+        nc.vector.tensor_copy(
+            out=z3_st[:].rearrange("p (u c i t) -> p u c t i", u=2, i=4, t=PACK),
+            in_=z1[:].rearrange("p (u t c i) -> p u c t i", u=2, i=4, t=PACK),
+        )
+        z3_codes = keep.tile([P, UNIT], U32, name="z3_codes", tag="y_st1", align_bytes=64)
+        z3_scales = keep.tile([P, UNIT], U8, name="z3_scales", align_bytes=64)
+        z3q = (z3_codes, z3_scales)
+        quantise(z3q, 0, z3_st[:])
 
         y3 = keep.tile([P, PACK, UNIT], F32, name="y3")
         for t in range(PACK):
-            product(last_banks[t][:], w3q, t, zq, last, False, True)
+            product(last_banks[t][:], w23q, PACK + t, z3q, slice(0, UNIT), False, True)
             if t % 2 == 0:
                 nc.scalar.activation(out=y3[:, t, :], in_=last_banks[t][:], func=RELU)
             else:

from contextlib import ExitStack

import concourse.mybir as mybir

K, T, H = 512, 512, 512
FLOPS = 3 * 2 * 512 * 512 * 512

F32 = mybir.dt.float32
BF16 = mybir.dt.bfloat16
I32 = mybir.dt.int32
U32 = mybir.dt.uint32
U16 = mybir.dt.uint16
U8 = mybir.dt.uint8
FP8X4 = mybir.dt.float8_e4m3fn_x4
RELU = mybir.ActivationFunctionType.Relu
COPY = mybir.ActivationFunctionType.Copy
MAX = mybir.AluOpType.max

P = 128
PACK = 4
UNIT = 128
SPARE = 192


def tile_picked_wsagecat_maxrelu_lo_kernel(
    tc, x_words, x_scales, w1, w2, w3, pos1, pos2, pos3, out_0, out_1, out_2
):
    nc = tc.nc
    with ExitStack() as ctx:
        keep = ctx.enter_context(tc.tile_pool(name="keep", bufs=1))
        psum = ctx.enter_context(tc.psum_pool(name="psum", bufs=1))

        def half(tag, width):
            return keep.tile([P, width], BF16, name=tag, tag=tag, align_bytes=64)

        def mx_tiles(name, width):
            codes = keep.tile([P, width], U32, name=name + "_codes", align_bytes=64)
            scales = keep.tile([P, width], U8, name=name + "_scales", align_bytes=64)
            return codes, scales

        def quantise(mx, first, staged):
            cols = slice(first, first + staged.shape[1] // PACK)
            nc.vector.quantize_mx(out=mx[0][:, cols].bitcast(FP8X4), scales=mx[1][:, cols], in_=staged)

        def product(acc, weights, t, moving, cols, start, stop):
            dealt = slice(P * t, P * (t + 1))
            nc.tensor.matmul_mx(
                out=acc,
                lhsT=weights[0][:, dealt].bitcast(FP8X4),
                lhsT_scale=weights[1][:, dealt],
                rhs=moving[0][:, cols].bitcast(FP8X4),
                rhs_scale=moving[1][:, cols],
                start=start,
                stop=stop,
            )

        w1_raw = [keep.tile([P, 2, H], F32, name="w1_raw%d" % i) for i in range(2)]
        raw = [keep.tile([P, PACK, H], F32, name="raw%d" % i) for i in range(2)]
        lists = [keep.tile([P, T // 16], U16, name="list%d" % i) for i in range(3)]
        xq = mx_tiles("x", T)
        for i in range(2):
            nc.sync.dma_start(out=w1_raw[i][:], in_=w1.rearrange("(p j) c -> p j c", j=PACK)[:, 2 * i : 2 * i + 2, :])
        scale_rows = x_scales[0].bitcast(I32)
        for q in range(4):
            nc.scalar.dma_start(
                out=xq[1][32 * q : 32 * (q + 1), :].bitcast(I32),
                in_=scale_rows[4 * q : 4 * q + 4, :].partition_broadcast(8),
            )
        nc.sync.dma_start(out=xq[0][:].bitcast(I32), in_=x_words[0].rearrange("p c r -> p (c r)").bitcast(I32))
        nc.sync.dma_start(lists[0][:], pos1)
        nc.sync.dma_start(lists[1][:], pos2)
        nc.sync.dma_start(lists[2][:], pos3)
        nc.sync.dma_start(out=raw[0][:], in_=w2.rearrange("(p j) c -> p j c", j=PACK))
        nc.sync.dma_start(out=raw[1][:], in_=w3.rearrange("(p j) c -> p j c", j=PACK))

        def deal_views(staged, source, t0, t1):
            dst = staged.rearrange("p (t m j) -> p m j t", t=t1 - t0, j=PACK)
            src = source[:].rearrange("p j (m t) -> p m j t", t=PACK)[:, :, :, t0:t1]
            return dst, src

        w1q = mx_tiles("w1", H)
        w1_st = [half("w1_st01", 2 * H), half("w1_st23", 2 * H)]
        for i in range(2):
            dst, src = deal_views(w1_st[1][:], w1_raw[i], 2, 4)
            nc.vector.tensor_copy(out=dst[:, :, 2 * i : 2 * i + 2, :], in_=src)
            dst, src = deal_views(w1_st[0][:], w1_raw[i], 0, 2)
            nc.scalar.activation(out=dst[:, :, 2 * i : 2 * i + 2, :], in_=src, func=COPY)
        quantise(w1q, 3 * P, w1_st[1][:, H : 2 * H])
        quantise(w1q, 2 * P, w1_st[1][:, 0:H])
        quantise(w1q, 0, w1_st[0][:])

        h_flat = keep.tile([P, PACK * T + SPARE], F32, name="h_flat")
        nc.gpsimd.memset(h_flat[:, PACK * T :], 0.0)
        h = h_flat[:, 0 : PACK * T].rearrange("p (t v) -> p t v", t=PACK)
        for a in range(2):
            cols = slice(a * T // 2, (a + 1) * T // 2)
            bank = psum.tile([P, T // 2], F32, name="h_bank", tag=("plane3", "spare")[a])
            product(bank[:], w1q, 3, xq, cols, True, True)
            nc.scalar.activation(out=h[:, 3, cols], in_=bank[:], func=RELU)
        for t in (2, 1, 0):
            bank = psum.tile([P, T], F32, name="h_bank", tag="plane%d" % t)
            product(bank[:], w1q, t, xq, slice(0, T), True, True)
            nc.scalar.activation(out=h[:, t, :], in_=bank[:], func=RELU)

        def weave_views(staged, planes):
            dst = staged.rearrange("p (c i t) -> p c t i", i=4, t=PACK)
            src = planes.rearrange("p t (c i) -> p c t i", i=4)
            return dst, src

        def gather(tile, d, t, first, n, run):
            dst = tile.rearrange("p (a t b) -> p a t b", b=run, t=PACK)[:, :, t, :]
            offsets = lists[d][:, first // 16 : (first + n) // 16]
            nc.vector.tensor_copy(out=dst, in_=h_flat[:, T * t : T * (t + 1) + (SPARE if n == T else 0)].indirect(offsets))

        hq = mx_tiles("h", T)
        zq = mx_tiles("z", 3 * UNIT)
        w23q = mx_tiles("w23", 2 * H)
        yq = mx_tiles("y", T)
        out_rows = out_0.rearrange("(p t) v -> p t v", t=PACK)
        word_rows = out_1[0].rearrange("p c r -> p (c r)").bitcast(I32)

        def unit(u, staged):
            cols = slice(UNIT * u, UNIT * (u + 1))
            bank = psum.tile([P, PACK, UNIT], F32, name="y_bank", tag="unit%d" % u)
            for t in range(PACK):
                product(bank[:, t, :], w23q, t, hq, cols, True, False)
                product(bank[:, t, :], w23q, PACK + t, zq, cols, False, True)
            y = keep.tile([P, PACK, UNIT], F32, name="y%d" % u)
            nc.scalar.activation(out=y[:], in_=bank[:], func=RELU)
            nc.sync.dma_start(out=out_rows[:, :, cols], in_=y[:])
            nc.scalar.activation(
                out=staged.rearrange("p (v t) -> p v t", t=PACK), in_=bank[:].rearrange("p t v -> p v t"), func=RELU
            )

        W = PACK * UNIT
        g0 = [half("g0_%d" % d, (4 if d == 0 else 3) * W) for d in range(3)]
        for t in (3, 2, 1, 0):
            for d in range(3):
                gather(g0[d][:], d, t, 0, (4 if d == 0 else 3) * UNIT, UNIT)
        pair = half("pair0", 3 * W)
        z = half("z0", 3 * W)
        parts = [slice(0, 2 * W), slice(2 * W, 3 * W)]
        for b in parts:
            nc.vector.tensor_tensor(out=pair[:, b], in0=g0[0][:, b], in1=g0[1][:, b], op=MAX)
        for b in parts:
            nc.vector.tensor_tensor(out=z[:, b], in0=pair[:, b], in1=g0[2][:, b], op=MAX)

        h_st = half("h_st", PACK * T)
        dst, src = weave_views(h_st[:], h)
        nc.scalar.copy(out=dst, in_=src)
        quantise(hq, 0, h_st[:])

        w23_st = half("w23_st", 2 * PACK * H)
        for i in range(2):
            dst, src = deal_views(w23_st[:, i * PACK * H : (i + 1) * PACK * H], raw[i], 0, 4)
            nc.scalar.activation(out=dst, in_=src, func=COPY)
        quantise(w23q, 0, w23_st[:])

        last = slice(3 * UNIT, 4 * UNIT)
        last_banks = [psum.tile([P, UNIT], F32, name="last_bank", tag="plane%d" % t) for t in range(PACK)]
        for t in range(PACK):
            product(last_banks[t][:], w23q, t, hq, last, True, False)

        z01_st = half("z01_st", 2 * W)
        nc.scalar.copy(
            out=z01_st[:].rearrange("p (u c i t) -> p u c t i", u=2, i=4, t=PACK),
            in_=z[:, parts[0]].rearrange("p (u t c i) -> p u c t i", u=2, i=4, t=PACK),
        )
        quantise(zq, 0, z01_st[:])
        z2_st = half("z2_st", W)
        dst, src = weave_views(z2_st[:], z[:, parts[1]].rearrange("p (t v) -> p t v", t=PACK))
        nc.scalar.copy(out=dst, in_=src)
        quantise(zq, 2 * UNIT, z2_st[:])

        y_st = [half("y_st%d" % u, W) for u in range(3)]
        for u in range(3):
            unit(u, y_st[u][:])
            quantise(yq, UNIT * u, y_st[u][:])
        nc.sync.dma_start(out=word_rows[:, 0:256], in_=yq[0][:, 0:256].bitcast(I32))

        g1 = [None, half("z01_st", W)[:], half("z2_st", W)[:]]
        for t in range(PACK):
            gather(g1[1], 1, t, 384, UNIT, UNIT // 2)
        pair1 = half("pair1", W)
        gather(g1[2], 2, 0, 384, UNIT, UNIT // 2)
        nc.vector.tensor_tensor(
            out=pair1[:].rearrange("p (a t b) -> p a t b", a=2, t=PACK),
            in0=g0[0][:, 3 * W : 4 * W].rearrange("p (t a b) -> p a t b", a=2, t=PACK),
            in1=g1[1].rearrange("p (a t b) -> p a t b", a=2, t=PACK),
            op=MAX,
        )
        for t in range(1, PACK):
            gather(g1[2], 2, t, 384, UNIT, UNIT // 2)
        z1 = half("z1", W)

        def planes(flat, t0, t1):
            return flat.rearrange("p (a t b) -> p a t b", a=2, t=PACK)[:, :, t0:t1, :]

        for t0, t1 in ((0, 3), (3, 4)):
            nc.vector.tensor_tensor(
                out=planes(z1[:], t0, t1), in0=planes(pair1[:], t0, t1), in1=planes(g1[2], t0, t1), op=MAX
            )
        z3_st = half("y_st0", W)
        nc.vector.tensor_copy(
            out=z3_st[:].rearrange("p (u c i t) -> p u c t i", u=2, i=4, t=PACK),
            in_=z1[:].rearrange("p (u t c i) -> p u c t i", u=2, i=4, t=PACK),
        )
        z3_codes = keep.tile([P, UNIT], U32, name="z3_codes", tag="y_st1", align_bytes=64)
        z3_scales = keep.tile([P, UNIT], U8, name="z3_scales", align_bytes=64)
        z3q = (z3_codes, z3_scales)
        quantise(z3q, 0, z3_st[:])

        y3 = keep.tile([P, PACK, UNIT], F32, name="y3")
        for t in range(PACK):
            product(last_banks[t][:], w23q, PACK + t, z3q, slice(0, UNIT), False, True)
            if t % 2 == 0:
                nc.scalar.activation(out=y3[:, t, :], in_=last_banks[t][:], func=RELU)
            else:
                nc.vector.tensor_scalar_max(out=y3[:, t, :], in0=last_banks[t][:], scalar1=0.0)
        nc.sync.dma_start(out=out_rows[:, :, last], in_=y3[:])
        y3_st = half("y3_st", PACK * UNIT)
        dst, src = weave_views(y3_st[:], y3[:])
        nc.vector.tensor_copy(out=dst, in_=src)
        quantise(yq, 384, y3_st[:])
        nc.sync.dma_start(out=word_rows[:, 256:512], in_=yq[0][:, 256:512].bitcast(I32))
        out_scale_rows = out_2[0].bitcast(I32)
        for q in range(4):
            queue = nc.scalar if q % 2 == 0 else nc.sync
            queue.dma_start(out=out_scale_rows[4 * q : 4 * q + 4, :], in_=yq[1][32 * q : 32 * q + 4, :].bitcast(I32))
